import numpy as np
import ml_dtypes


def mxq(x, axis, fmt="e4m3"):
    dtype, down = {"e4m3": (ml_dtypes.float8_e4m3fn, 7), "e5m2": (ml_dtypes.float8_e5m2, 14)}[fmt]
    v = np.moveaxis(np.asarray(x, np.float32).astype(ml_dtypes.bfloat16).astype(np.float64), axis, -1)
    blocks = v.reshape(v.shape[:-1] + (-1, 32))
    amax = np.abs(blocks).max(-1, keepdims=True)
    byte = np.maximum(np.where(amax > 0, np.frexp(amax)[1] - 1 + 127, 0) - down, 1)
    scale = np.exp2(byte - 127.0)
    codes = (blocks / scale).astype(np.float32).astype(dtype).astype(np.float64)
    return np.moveaxis((codes * scale).reshape(v.shape), -1, axis)


WIDE = False


def mx_kscale(k):
    if not WIDE:
        return np.ones(k)
    levels = np.array([10, -10, 5, -5, 0])
    if k % 512:
        return np.exp2(np.random.permutation(np.resize(levels, k // 32))).repeat(32)
    a = np.empty((k // 512, 16))
    for p in range(k // 512):
        a[p, :8] = np.random.permutation(np.resize(levels, 8))
        for g in range(8):
            far = levels[np.abs(levels - a[p, g]) >= 10]
            a[p, g + 8] = far[np.random.randint(len(far))]
    return np.exp2(a.ravel()).repeat(32)


BF16 = ml_dtypes.bfloat16


def bf(x):
    return np.asarray(x, np.float32).astype(BF16)


def f64(x):
    return np.asarray(x).astype(np.float64)


B, P, V = 1024, 1536, 512


def setup_inputs():
    s = mx_kscale(P)
    u = mx_kscale(B)
    t = mx_kscale(P)
    return {
        "x": bf(np.random.standard_normal((B, P)) * s * u[:, None]),
        "sub": bf(0.5 * np.random.standard_normal((P, P)) / np.sqrt(P) / s[:, None] * t),
        "hold": bf((1 + 0.1 * np.random.standard_normal(P)) / s * t),
        "cont": bf(0.35 * np.random.standard_normal((B, B)) / np.sqrt(B) / u),
        "keep": bf((1 + 0.1 * np.random.standard_normal(B)) / u),
        "dbl": bf(np.random.standard_normal((P, V)) / np.sqrt(P) / t[:, None]),
        "gain": bf(1 + 0.1 * np.random.standard_normal(V)),
    }


def reference(x, sub, hold, cont, keep, dbl, gain):
    x = f64(x)
    r = mxq(x, 1, "e4m3") @ mxq(f64(sub), 0, "e4m3")
    h = x * f64(hold) + np.maximum(r, 0.0)
    m = mxq(f64(cont), 1, "e4m3") @ mxq(h, 0, "e4m3")
    c = h * f64(keep)[:, None] + m
    y = mxq(c, 1, "e4m3") @ mxq(f64(dbl), 0, "e4m3")
    return y * f64(gain)

@@ -1,0 +1,340 @@
+from contextlib import ExitStack
+
+import concourse.mybir as mybir
+from concourse.masks import make_identity
+
+B, PITCH, V = 1024, 1536, 512
+FLOPS = 2 * (B * PITCH * PITCH + B * B * PITCH + B * PITCH * V)
+
+F32 = mybir.dt.float32
+BF16 = mybir.dt.bfloat16
+U32 = mybir.dt.uint32
+U8 = mybir.dt.uint8
+FP8X4 = mybir.dt.float8_e4m3fn_x4
+ALU = mybir.AluOpType
+
+P = 128
+T = 4
+K_PASS = P * T
+NG = B // K_PASS
+NC = PITCH // K_PASS
+MANUAL = False
+
+
+def tile_chord_substitution_continuity_doubli_t1_kernel(tc, x, sub, hold, cont, keep, dbl, gain, out):
+    nc = tc.nc
+    with ExitStack() as ctx:
+        const = ctx.enter_context(tc.tile_pool(name="const", bufs=1))
+        res = ctx.enter_context(tc.tile_pool(name="res", bufs=1))
+        work = ctx.enter_context(tc.tile_pool(name="work", bufs=2))
+        psum = ctx.enter_context(tc.psum_pool(name="psum", bufs=4))
+        if MANUAL:
+            ctx.enter_context(tc.manual_schedule())
+
+        x_v = x.rearrange("(g p t) k -> g p t k", g=NG, t=T)
+        cont_v = cont.rearrange("(g p t) k -> g p t k", g=NG, t=T)
+        sub_v = sub.rearrange("(c p j) w -> c p j w", c=NC, j=T)
+        dbl_v = dbl.rearrange("(c p j) w -> c p j w", c=NC, j=T)
+        out_v = out.rearrange("(g p t) w -> g p t w", g=NG, t=T)
+
+        ident = const.tile([P, P], F32, name="ident")
+        hold_b = const.tile([P, PITCH], BF16, name="hold_b")
+        gain_b = const.tile([P, V], BF16, name="gain_b")
+        keep_b = const.tile([P, NG, T], BF16, name="keep_b")
+        warm = const.tile([P, 2], F32, name="warm")
+
+        xr, sr, cr = {}, {}, {}
+
+        def load_x(g, pr):
+            t = res.tile([P, 2, PITCH], BF16, name=f"xr{g}{pr}", tag=f"xr{g}{pr}")
+            nc.sync.dma_start(out=t[:], in_=x_v[g][:, 2 * pr : 2 * pr + 2, :])
+            xr[g, pr] = t
+
+        def load_hold(n):
+            nc.sync.dma_start(
+                out=hold_b[:, n * K_PASS : (n + 1) * K_PASS],
+                in_=hold[n * K_PASS : (n + 1) * K_PASS].partition_broadcast(P),
+            )
+
+        def load_piece(n, c):
+            t = work.tile([P, T, K_PASS], BF16, name=f"raw{n}{c}", tag="raw", bufs=10)
+            nc.sync.dma_start(out=t[:], in_=sub_v[c][:, :, n * K_PASS : (n + 1) * K_PASS] if n < NC else dbl_v[c])
+            sr[n, c] = t[:]
+
+        def load_cont(g, pr):
+            t = work.tile([P, 2, B], BF16, name=f"cr{g}{pr}", tag="raw", bufs=10)
+            nc.sync.dma_start(out=t[:], in_=cont_v[g][:, 2 * pr : 2 * pr + 2, :])
+            cr[g, pr] = t
+
+        def codes(key, tag, bufs):
+            q = work.tile([P, K_PASS], U32, name="q" + key, tag="q" + tag, bufs=bufs, align_bytes=64)
+            s = work.tile([P, K_PASS], U8, name="s" + key, tag="s" + tag, bufs=bufs, align_bytes=64)
+            return q, s
+
+        def grouped(key):
+            return work.tile([P, K_PASS, T], BF16, name="g" + key, tag="grouped", bufs=8, align_bytes=64)
+
+        def quantize(g, q):
+            nc.vector.quantize_mx(
+                out=q[0][:].bitcast(FP8X4), scales=q[1][:], in_=g[:].rearrange("p r j -> p (r j)")
+            )
+
+        def mx(acc, lhs, m0, rhs, start, stop):
+            nc.tensor.matmul_mx(
+                out=acc[:],
+                lhsT=lhs[0][:, m0 : m0 + P].bitcast(FP8X4),
+                lhsT_scale=lhs[1][:, m0 : m0 + P],
+                rhs=rhs[0][:].bitcast(FP8X4),
+                rhs_scale=rhs[1][:],
+                start=start,
+                stop=stop,
+            )
+
+        ys, gx, xq, gc, cq, gs, sq, h, gh, hq, cb, gq, dq = {}, {}, {}, {}, {}, {}, {}, {}, {}, {}, {}, {}, {}
+
+        def turn(words, key, dst, dst_q, pr, step):
+            bank = psum.tile([P, 2, 2 * P], F32, name="tp" + key, tag="tp")
+            for tt in range(2):
+                for u in range(2):
+                    w = words[tt]
+                    src = w[:, u : 2 * P : 2] if step == 2 else w[:, u * P : (u + 1) * P]
+                    nc.tensor.transpose(bank[:, u, tt * P : (tt + 1) * P], src, ident[:])
+            nc.scalar.copy(
+                out=dst[:].rearrange("p r j -> p (r j)").bitcast(F32).rearrange("p (r u) -> p r u", u=2)[
+                    :, pr * 2 * P : (pr + 1) * 2 * P, :
+                ],
+                in_=bank[:].rearrange("p u r -> p r u"),
+            )
+
+        def turn_x(g, pr, c):
+            if (g, c) not in gx:
+                gx[g, c] = grouped(f"x{g}{c}")
+            w = [xr[g, pr][:, tt, c * K_PASS : (c + 1) * K_PASS].bitcast(F32) for tt in range(2)]
+            turn(w, f"x{g}{pr}{c}", gx[g, c], None, pr, 2)
+
+        def q_x(g, c):
+            xq[g, c] = codes(f"x{g}{c}", "x", 6)
+            quantize(gx[g, c], xq[g, c])
+
+        def turn_cont(go, gi, pr):
+            if (go, gi) not in gc:
+                gc[go, gi] = grouped(f"c{go}{gi}")
+            w = [cr[go, pr][:, tt, gi * K_PASS : (gi + 1) * K_PASS].bitcast(F32) for tt in range(2)]
+            turn(w, f"c{go}{gi}{pr}", gc[go, gi], None, pr, 2)
+
+        def q_cont(go, gi):
+            cq[go, gi] = codes(f"c{go}{gi}", "c", 4)
+            quantize(gc[go, gi], cq[go, gi])
+
+        def inter(n, c, eng):
+            gs[n, c] = grouped(f"s{n}{c}")
+            if n < 3:
+                for u in range(2):
+                    o = gs[n, c][:, u * 2 * P : (u + 1) * 2 * P, :].rearrange("p (q e) j -> p q j e", e=2)
+                    i = sr[n, c].rearrange("p j (q v e) -> p v q j e", v=2, e=2)[:, u]
+                    if eng == "v":
+                        nc.vector.tensor_copy(out=o, in_=i)
+                    else:
+                        nc.scalar.copy(out=o, in_=i)
+            else:
+                for k in range(4):
+                    cols = slice(k * (K_PASS // 4), (k + 1) * (K_PASS // 4))
+                    o = gs[n, c][:, cols, :].rearrange("p (q i) j -> p q j i", i=4)
+                    i = sr[n, c][:, :, cols].rearrange("p j (q i) -> p q j i", i=4)
+                    if eng == "v":
+                        nc.vector.tensor_copy(out=o, in_=i)
+                    else:
+                        nc.scalar.copy(out=o, in_=i)
+
+        def q_s(n, c):
+            sq[n, c] = codes(f"s{n}{c}", "s" if n < 3 else "d", 6 if n < 3 else 3)
+            quantize(gs[n, c], sq[n, c])
+
+        def held(n, g, t):
+            eng = nc.gpsimd if (False) else nc.vector
+            if (n, g) not in h:
+                h[n, g] = work.tile([P, T, K_PASS], F32, name=f"h{n}{g}", tag="h", bufs=6)
+            eng.tensor_tensor(
+                out=h[n, g][:, t, :].rearrange("p (v q e) -> p v q e", v=2, e=2),
+                in0=xr[g, t // 2][:, t % 2, n * K_PASS : (n + 1) * K_PASS].rearrange("p (q v e) -> p v q e", v=2, e=2),
+                in1=hold_b[:, n * K_PASS : (n + 1) * K_PASS].rearrange("p (q v e) -> p v q e", v=2, e=2),
+                op=ALU.mult,
+            )
+
+        def acc_tile(key):
+            return psum.tile([P, K_PASS], F32, name="acc" + key, tag="acc")
+
+        def add_relu(n, g, t, acc):
+            nc.vector.scalar_tensor_tensor(
+                out=h[n, g][:, t, :], in0=acc[:], scalar=0.0, in1=h[n, g][:, t, :], op0=ALU.max, op1=ALU.add
+            )
+
+        def s1(n, g, t):
+            acc = acc_tile(f"r{n}{g}{t}")
+            for c in range(NC):
+                mx(acc, xq[g, c], t * P, sq[n, c], c == 0, c == NC - 1)
+            add_relu(n, g, t, acc)
+
+        def cast_h(n, g):
+            gh[n, g] = grouped(f"h{n}{g}")
+            for half in range(2):
+                lo, hi = half * 2 * P, (half + 1) * 2 * P
+                nc.scalar.copy(
+                    out=gh[n, g][:, lo:hi, :].rearrange("p (q i) t -> p q t i", i=4),
+                    in_=h[n, g][:, :, lo:hi].rearrange("p t (q i) -> p q t i", i=4),
+                )
+
+        def q_h(n, g):
+            hq[n, g] = codes(f"h{n}{g}", "h", 4)
+            quantize(gh[n, g], hq[n, g])
+
+        def s2(n, go, t):
+            acc = acc_tile(f"m{n}{go}{t}")
+            for gi in range(NG):
+                mx(acc, cq[go, gi], t * P, hq[n, gi], gi == 0, gi == NG - 1)
+            if (n, go) not in cb:
+                cb[n, go] = work.tile([P, T, K_PASS], BF16, name=f"cb{n}{go}", tag="cb", bufs=2)
+            nc.vector.scalar_tensor_tensor(
+                out=cb[n, go][:, t, :],
+                in0=h[n, go][:, t, :],
+                scalar=keep_b[:, go, t : t + 1],
+                in1=acc[:],
+                op0=ALU.mult,
+                op1=ALU.add,
+            )
+
+        def turn_c(n, go, pr):
+            if (n, go) not in gq:
+                gq[n, go] = grouped(f"q{n}{go}")
+            w = [cb[n, go][:, 2 * pr + tt, :].bitcast(F32) for tt in range(2)]
+            turn(w, f"q{n}{go}{pr}", gq[n, go], None, pr, 1)
+
+        def q_c(n, go):
+            dq[n, go] = codes(f"q{n}{go}", "q", 6)
+            quantize(gq[n, go], dq[n, go])
+
+        def s3(go, t):
+            acc = acc_tile(f"y{go}{t}")
+            for n in range(NC):
+                mx(acc, dq[n, go], t * P, sq[3, n], n == 0, n == NC - 1)
+            if go not in ys:
+                ys[go] = work.tile([P, T, V], F32, name=f"y{go}", tag="h", bufs=6)
+            nc.vector.tensor_tensor(out=ys[go][:, t, :], in0=acc[:], in1=gain_b[:], op=ALU.mult)
+            nc.sync.dma_start(out=out_v[go][:, t, :], in_=ys[go][:, t, :])
+
+        G = nc.gpsimd
+        loads = (
+            [(load_x, 0, 0), (load_hold, 0), (load_hold, 1), (load_x, 0, 1)]
+            + [(load_piece, 0, c) for c in range(NC)]
+            + [(load_x, 1, 0), (load_x, 1, 1)]
+            + [(load_piece, 1, c) for c in range(NC)]
+            + [(load_cont, 0, 0), (load_cont, 0, 1), (load_cont, 1, 0), (load_cont, 1, 1)]
+        )
+        for f, *a in loads:
+            f(*a)
+        nc.sync.dma_start(out=keep_b[:], in_=keep.rearrange("(g p t) -> p g t", g=NG, t=T))
+        nc.sync.dma_start(out=gain_b[:], in_=gain.partition_broadcast(P))
+
+        nc.vector.memset(warm[:], 0.0)
+        nc.scalar.copy(out=warm[:, 0:1], in_=warm[:, 1:2])
+        make_identity(nc, ident[:])
+
+
+        for pr in range(2):
+            for c in range(NC):
+                turn_x(0, pr, c)
+            held(0, 0, 2 * pr)
+            held(0, 0, 2 * pr + 1)
+            if pr == 0:
+                held(1, 0, 0)
+                held(1, 0, 1)
+        inter(0, 0, "v")
+        inter(0, 1, "s")
+        inter(0, 2, "s")
+        q_x(0, 0)
+        q_s(0, 0)
+        q_x(0, 1)
+        q_x(0, 2)
+        held(1, 0, 2)
+        q_s(0, 1)
+        held(1, 0, 3)
+        held(0, 1, 0)
+        held(0, 1, 1)
+        q_s(0, 2)
+        acc0 = [acc_tile(f"r00{t}") for t in range(T)]
+        for c in range(NC):
+            for t in range(T):
+                mx(acc0[t], xq[0, c], t * P, sq[0, c], c == 0, c == NC - 1)
+        for pr in range(2):
+            for c in range(NC):
+                turn_x(1, pr, c)
+        for t in range(T):
+            add_relu(0, 0, t, acc0[t])
+        held(0, 1, 2)
+        held(0, 1, 3)
+        for c in range(NC):
+            load_piece(2, c)
+        for c in range(NC):
+            q_x(1, c)
+        inter(1, 0, "s")
+        cast_h(0, 0)
+        inter(1, 1, "s")
+        for t in range(T):
+            s1(0, 1, t)
+            held(1, 1, t)
+        q_h(0, 0)
+        q_s(1, 0)
+        inter(1, 2, "s")
+        q_s(1, 1)
+        for go in range(NG):
+            for pr in range(2):
+                for gi in range(NG):
+                    turn_cont(go, gi, pr)
+            if go == 0:
+                cast_h(0, 1)
+        q_s(1, 2)
+        tiles = [(g, t) for g in range(NG) for t in range(T)]
+        at = {}
+
+        def later(i, f, *a):
+            at.setdefault(i, []).append((f, a))
+
+        for n in range(1, NC + 1):
+            s = 8 * n
+            if n < NC:
+                for g in range(NG):
+                    later(s + 4 * g + 3, cast_h, n, g)
+                    later(s + 4 * g + 3 + 2, q_h, n, g)
+            if n + 1 < NC:
+                for c in range(NC):
+                    later(s + 0 + 2 * c, inter, n + 1, c, "s")
+                    later(s + 0 + 2 * c + 1, q_s, n + 1, c)
+            if n + 1 < NC:
+                for k, (g, t) in enumerate(tiles):
+                    later(s + k, held, n + 1, g, t)
+            for g in range(NG):
+                for pr in range(2):
+                    later(s + 3 + 4 * g + 2 * pr + 1 + 2, turn_c, n - 1, g, pr)
+                later(s + 3 + 4 * g + 3 + 2 + 1, q_c, n - 1, g)
+        for c in range(NC):
+            later(27 + 1 * c, inter, 3, c, "s")
+            later(27 + 1 * c + 1, q_s, 3, c)
+        later(8, q_cont, 0, 0)
+        later(8, q_cont, 0, 1)
+        later(9, q_h, 0, 1)
+        later(10, q_cont, 1, 0)
+        later(10, q_cont, 1, 1)
+        for c in range(NC):
+            later(12, load_piece, 3, c)
+        load_hold(2)
+        for i in range(8, 8 * (NC + 1) + 3 + 2 + 1 + 1):
+            if i < 8 * NC:
+                s1(i // 8, *tiles[i % 8])
+            j = i - 8 - 3
+            if 0 <= j < 8 * NC:
+                s2(j // 8, *tiles[j % 8])
+            for f, a in at.get(i, []):
+                f(*a)
+        for go in range(NG):
+            for t in range(T):
+                s3(go, t)

@@ -18,6 +18,8 @@ T = 4
 K_PASS = P * T
 NG = B // K_PASS
 NC = PITCH // K_PASS
+HR = PITCH // P
+GR = V // P
 MANUAL = False
 
 
@@ -27,7 +29,7 @@ def tile_chord_substitution_continuity_doubli_t1_kernel(tc, x, sub, hold, cont, 
         const = ctx.enter_context(tc.tile_pool(name="const", bufs=1))
         res = ctx.enter_context(tc.tile_pool(name="res", bufs=1))
         work = ctx.enter_context(tc.tile_pool(name="work", bufs=2))
-        psum = ctx.enter_context(tc.psum_pool(name="psum", bufs=4))
+        psum = ctx.enter_context(tc.psum_pool(name="psum", bufs=8))
         if MANUAL:
             ctx.enter_context(tc.manual_schedule())
 
@@ -50,11 +52,27 @@ def tile_chord_substitution_continuity_doubli_t1_kernel(tc, x, sub, hold, cont, 
             nc.sync.dma_start(out=t[:], in_=x_v[g][:, 2 * pr : 2 * pr + 2, :])
             xr[g, pr] = t
 
-        def load_hold(n):
-            nc.sync.dma_start(
-                out=hold_b[:, n * K_PASS : (n + 1) * K_PASS],
-                in_=hold[n * K_PASS : (n + 1) * K_PASS].partition_broadcast(P),
-            )
+        rows = const.tile([P, P], BF16, name="rows")
+        cols_b = const.tile([P, P], BF16, name="cols_b")
+        ident_b = const.tile([P, P], BF16, name="ident_b")
+
+        def load_rows():
+            nc.sync.dma_start(out=rows[0:HR, :], in_=hold.rearrange("(c p) -> c p", p=P))
+            nc.sync.dma_start(out=rows[HR : HR + GR, :], in_=gain.rearrange("(c p) -> c p", p=P))
+
+        def spread_rows():
+            bank = psum.tile([P, P], BF16, name="rt", tag="bank")
+            nc.tensor.transpose(bank[:], rows[:], ident_b[:])
+            nc.scalar.copy(out=cols_b[:], in_=bank[:])
+            for k in range(NC + 1):
+                bank = psum.tile([P, K_PASS], BF16, name=f"rb{k}", tag="bank")
+                for i in range(T):
+                    c = T * k + i
+                    nc.tensor.transpose(
+                        bank[:, i * P : (i + 1) * P], cols_b[:, c : c + 1].to_broadcast([P, P]), ident_b[:]
+                    )
+                dst = hold_b[:, k * K_PASS : (k + 1) * K_PASS] if k < NC else gain_b[:]
+                nc.scalar.copy(out=dst, in_=bank[:])
 
         def load_piece(n, c):
             t = work.tile([P, T, K_PASS], BF16, name=f"raw{n}{c}", tag="raw", bufs=10)
@@ -93,7 +111,7 @@ def tile_chord_substitution_continuity_doubli_t1_kernel(tc, x, sub, hold, cont, 
         ys, gx, xq, gc, cq, gs, sq, h, gh, hq, cb, gq, dq = {}, {}, {}, {}, {}, {}, {}, {}, {}, {}, {}, {}, {}
 
         def turn(words, key, dst, dst_q, pr, step):
-            bank = psum.tile([P, 2, 2 * P], F32, name="tp" + key, tag="tp")
+            bank = psum.tile([P, 2, 2 * P], F32, name="tp" + key, tag="bank")
             for tt in range(2):
                 for u in range(2):
                     w = words[tt]
@@ -128,17 +146,9 @@ def tile_chord_substitution_continuity_doubli_t1_kernel(tc, x, sub, hold, cont, 
 
         def inter(n, c, eng):
             gs[n, c] = grouped(f"s{n}{c}")
-            if n < 3:
-                for u in range(2):
-                    o = gs[n, c][:, u * 2 * P : (u + 1) * 2 * P, :].rearrange("p (q e) j -> p q j e", e=2)
-                    i = sr[n, c].rearrange("p j (q v e) -> p v q j e", v=2, e=2)[:, u]
-                    if eng == "v":
-                        nc.vector.tensor_copy(out=o, in_=i)
-                    else:
-                        nc.scalar.copy(out=o, in_=i)
-            else:
-                for k in range(4):
-                    cols = slice(k * (K_PASS // 4), (k + 1) * (K_PASS // 4))
+            if True:
+                for k in range(2):
+                    cols = slice(k * (K_PASS // 2), (k + 1) * (K_PASS // 2))
                     o = gs[n, c][:, cols, :].rearrange("p (q i) j -> p q j i", i=4)
                     i = sr[n, c][:, :, cols].rearrange("p j (q i) -> p q j i", i=4)
                     if eng == "v":
@@ -150,19 +160,21 @@ def tile_chord_substitution_continuity_doubli_t1_kernel(tc, x, sub, hold, cont, 
             sq[n, c] = codes(f"s{n}{c}", "s" if n < 3 else "d", 6 if n < 3 else 3)
             quantize(gs[n, c], sq[n, c])
 
-        def held(n, g, t):
-            eng = nc.gpsimd if (False) else nc.vector
+        def held(n, g, pr):
             if (n, g) not in h:
                 h[n, g] = work.tile([P, T, K_PASS], F32, name=f"h{n}{g}", tag="h", bufs=6)
+            cols = slice(n * K_PASS, (n + 1) * K_PASS)
+            eng = nc.gpsimd if (False) else nc.vector
             eng.tensor_tensor(
-                out=h[n, g][:, t, :].rearrange("p (v q e) -> p v q e", v=2, e=2),
-                in0=xr[g, t // 2][:, t % 2, n * K_PASS : (n + 1) * K_PASS].rearrange("p (q v e) -> p v q e", v=2, e=2),
-                in1=hold_b[:, n * K_PASS : (n + 1) * K_PASS].rearrange("p (q v e) -> p v q e", v=2, e=2),
+                out=h[n, g][:, 2 * pr : 2 * pr + 2, :],
+                in0=xr[g, pr][:, :, cols],
+                in1=hold_b[:, cols].unsqueeze(1).to_broadcast([P, 2, K_PASS]),
                 op=ALU.mult,
             )
 
+
         def acc_tile(key):
-            return psum.tile([P, K_PASS], F32, name="acc" + key, tag="acc")
+            return psum.tile([P, K_PASS], F32, name="acc" + key, tag="bank")
 
         def add_relu(n, g, t, acc):
             nc.vector.scalar_tensor_tensor(
@@ -207,24 +219,31 @@ def tile_chord_substitution_continuity_doubli_t1_kernel(tc, x, sub, hold, cont, 
             if (n, go) not in gq:
                 gq[n, go] = grouped(f"q{n}{go}")
             w = [cb[n, go][:, 2 * pr + tt, :].bitcast(F32) for tt in range(2)]
-            turn(w, f"q{n}{go}{pr}", gq[n, go], None, pr, 1)
+            turn(w, f"q{n}{go}{pr}", gq[n, go], None, pr, 2)
 
         def q_c(n, go):
             dq[n, go] = codes(f"q{n}{go}", "q", 6)
             quantize(gq[n, go], dq[n, go])
 
-        def s3(go, t):
-            acc = acc_tile(f"y{go}{t}")
-            for n in range(NC):
-                mx(acc, dq[n, go], t * P, sq[3, n], n == 0, n == NC - 1)
+        ay = {}
+
+        def s3_part(go, t, passes):
+            if passes[0] == 0:
+                ay[go, t] = acc_tile(f"y{go}{t}")
+            for n in passes:
+                mx(ay[go, t], dq[n, go], t * P, sq[3, n], n == 0, n == NC - 1)
+
+        def s3_out(go, t):
             if go not in ys:
                 ys[go] = work.tile([P, T, V], F32, name=f"y{go}", tag="h", bufs=6)
-            nc.vector.tensor_tensor(out=ys[go][:, t, :], in0=acc[:], in1=gain_b[:], op=ALU.mult)
+            nc.vector.tensor_tensor(out=ys[go][:, t, :], in0=ay[go, t][:], in1=gain_b[:], op=ALU.mult)
             nc.sync.dma_start(out=out_v[go][:, t, :], in_=ys[go][:, t, :])
 
         G = nc.gpsimd
+        nc.vector.memset(rows[:], 0.0)
+        load_rows()
         loads = (
-            [(load_x, 0, 0), (load_hold, 0), (load_hold, 1), (load_x, 0, 1)]
+            [(load_x, 0, 0), (load_x, 0, 1)]
             + [(load_piece, 0, c) for c in range(NC)]
             + [(load_x, 1, 0), (load_x, 1, 1)]
             + [(load_piece, 1, c) for c in range(NC)]
@@ -233,21 +252,20 @@ def tile_chord_substitution_continuity_doubli_t1_kernel(tc, x, sub, hold, cont, 
         for f, *a in loads:
             f(*a)
         nc.sync.dma_start(out=keep_b[:], in_=keep.rearrange("(g p t) -> p g t", g=NG, t=T))
-        nc.sync.dma_start(out=gain_b[:], in_=gain.partition_broadcast(P))
 
         nc.vector.memset(warm[:], 0.0)
         nc.scalar.copy(out=warm[:, 0:1], in_=warm[:, 1:2])
+        make_identity(nc, ident_b[:])
         make_identity(nc, ident[:])
+        spread_rows()
 
 
         for pr in range(2):
             for c in range(NC):
                 turn_x(0, pr, c)
-            held(0, 0, 2 * pr)
-            held(0, 0, 2 * pr + 1)
+            held(0, 0, pr)
             if pr == 0:
                 held(1, 0, 0)
-                held(1, 0, 1)
         inter(0, 0, "v")
         inter(0, 1, "s")
         inter(0, 2, "s")
@@ -255,11 +273,9 @@ def tile_chord_substitution_continuity_doubli_t1_kernel(tc, x, sub, hold, cont, 
         q_s(0, 0)
         q_x(0, 1)
         q_x(0, 2)
-        held(1, 0, 2)
         q_s(0, 1)
-        held(1, 0, 3)
+        held(1, 0, 1)
         held(0, 1, 0)
-        held(0, 1, 1)
         q_s(0, 2)
         acc0 = [acc_tile(f"r00{t}") for t in range(T)]
         for c in range(NC):
@@ -270,8 +286,7 @@ def tile_chord_substitution_continuity_doubli_t1_kernel(tc, x, sub, hold, cont, 
                 turn_x(1, pr, c)
         for t in range(T):
             add_relu(0, 0, t, acc0[t])
-        held(0, 1, 2)
-        held(0, 1, 3)
+        held(0, 1, 1)
         for c in range(NC):
             load_piece(2, c)
         for c in range(NC):
@@ -281,7 +296,8 @@ def tile_chord_substitution_continuity_doubli_t1_kernel(tc, x, sub, hold, cont, 
         inter(1, 1, "s")
         for t in range(T):
             s1(0, 1, t)
-            held(1, 1, t)
+            if t % 2 == 0:
+                held(1, 1, t // 2)
         q_h(0, 0)
         q_s(1, 0)
         inter(1, 2, "s")
@@ -310,15 +326,18 @@ def tile_chord_substitution_continuity_doubli_t1_kernel(tc, x, sub, hold, cont, 
                     later(s + 0 + 2 * c, inter, n + 1, c, "s")
                     later(s + 0 + 2 * c + 1, q_s, n + 1, c)
             if n + 1 < NC:
-                for k, (g, t) in enumerate(tiles):
-                    later(s + k, held, n + 1, g, t)
+                for g in range(NG):
+                    for pr in range(2):
+                        later(s + 0 + 4 * g + 2 * pr, held, n + 1, g, pr)
             for g in range(NG):
                 for pr in range(2):
-                    later(s + 3 + 4 * g + 2 * pr + 1 + 2, turn_c, n - 1, g, pr)
+                    later(s + 3 + 4 * g + (2 * pr + 1 if n == NC and g == 1 else 3) + 2, turn_c, n - 1, g, pr)
                 later(s + 3 + 4 * g + 3 + 2 + 1, q_c, n - 1, g)
+        for t in range(T):
+            later(35 + t // 4, s3_part, 0, t, [0, 1])
         for c in range(NC):
-            later(27 + 1 * c, inter, 3, c, "s")
-            later(27 + 1 * c + 1, q_s, 3, c)
+            later(26 + 1 * c, inter, 3, c, "s")
+            later(26 + 1 * c + 1, q_s, 3, c)
         later(8, q_cont, 0, 0)
         later(8, q_cont, 0, 1)
         later(9, q_h, 0, 1)
@@ -326,7 +345,6 @@ def tile_chord_substitution_continuity_doubli_t1_kernel(tc, x, sub, hold, cont, 
         later(10, q_cont, 1, 1)
         for c in range(NC):
             later(12, load_piece, 3, c)
-        load_hold(2)
         for i in range(8, 8 * (NC + 1) + 3 + 2 + 1 + 1):
             if i < 8 * NC:
                 s1(i // 8, *tiles[i % 8])
@@ -335,6 +353,11 @@ def tile_chord_substitution_continuity_doubli_t1_kernel(tc, x, sub, hold, cont, 
                 s2(j // 8, *tiles[j % 8])
             for f, a in at.get(i, []):
                 f(*a)
-        for go in range(NG):
-            for t in range(T):
-                s3(go, t)
+        for t in range(T):
+            s3_part(0, t, [2])
+            s3_out(0, t)
+        for t in range(T):
+            s3_part(1, t, [0, 1])
+        for t in range(T):
+            s3_part(1, t, [2])
+            s3_out(1, t)

@@ -3,8 +3,8 @@ from contextlib import ExitStack
 import concourse.mybir as mybir
 from concourse.masks import make_identity
 
-B, PITCH, V = 1024, 1536, 512
-FLOPS = 2 * (B * PITCH * PITCH + B * B * PITCH + B * PITCH * V)
+BARS, PITCHES, VOICES = 1024, 1536, 512
+FLOPS = 2 * (BARS * PITCHES * PITCHES + BARS * BARS * PITCHES + BARS * PITCHES * VOICES)
 
 F32 = mybir.dt.float32
 BF16 = mybir.dt.bfloat16
@@ -14,350 +14,351 @@ FP8X4 = mybir.dt.float8_e4m3fn_x4
 ALU = mybir.AluOpType
 
 P = 128
-T = 4
-K_PASS = P * T
-NG = B // K_PASS
-NC = PITCH // K_PASS
-HR = PITCH // P
-GR = V // P
-MANUAL = False
+SLOTS = 4
+PASS = P * SLOTS
+GROUPS = BARS // PASS
+CHUNKS = PITCHES // PASS
+DBL = CHUNKS
+BOTH = range(2)
 
 
 def tile_chord_substitution_continuity_doubli_t1_kernel(tc, x, sub, hold, cont, keep, dbl, gain, out):
     nc = tc.nc
     with ExitStack() as ctx:
         const = ctx.enter_context(tc.tile_pool(name="const", bufs=1))
-        res = ctx.enter_context(tc.tile_pool(name="res", bufs=1))
         work = ctx.enter_context(tc.tile_pool(name="work", bufs=2))
         psum = ctx.enter_context(tc.psum_pool(name="psum", bufs=8))
-        if MANUAL:
-            ctx.enter_context(tc.manual_schedule())
+        ctx.enter_context(tc.manual_schedule())
 
-        x_v = x.rearrange("(g p t) k -> g p t k", g=NG, t=T)
-        cont_v = cont.rearrange("(g p t) k -> g p t k", g=NG, t=T)
-        sub_v = sub.rearrange("(c p j) w -> c p j w", c=NC, j=T)
-        dbl_v = dbl.rearrange("(c p j) w -> c p j w", c=NC, j=T)
-        out_v = out.rearrange("(g p t) w -> g p t w", g=NG, t=T)
+        x_rows = x.rearrange("(g p t) k -> g p t k", g=GROUPS, t=SLOTS)
+        cont_rows = cont.rearrange("(g p t) k -> g p t k", g=GROUPS, t=SLOTS)
+        out_rows = out.rearrange("(g p t) v -> g p t v", g=GROUPS, t=SLOTS)
+        sub_rows = sub.rearrange("(c p j) w -> c p j w", c=CHUNKS, j=SLOTS)
+        dbl_rows = dbl.rearrange("(c p j) v -> c p j v", c=CHUNKS, j=SLOTS)
 
         ident = const.tile([P, P], F32, name="ident")
-        hold_b = const.tile([P, PITCH], BF16, name="hold_b")
-        gain_b = const.tile([P, V], BF16, name="gain_b")
-        keep_b = const.tile([P, NG, T], BF16, name="keep_b")
-        warm = const.tile([P, 2], F32, name="warm")
-
-        xr, sr, cr = {}, {}, {}
-
-        def load_x(g, pr):
-            t = res.tile([P, 2, PITCH], BF16, name=f"xr{g}{pr}", tag=f"xr{g}{pr}")
-            nc.sync.dma_start(out=t[:], in_=x_v[g][:, 2 * pr : 2 * pr + 2, :])
-            xr[g, pr] = t
-
-        rows = const.tile([P, P], BF16, name="rows")
-        cols_b = const.tile([P, P], BF16, name="cols_b")
         ident_b = const.tile([P, P], BF16, name="ident_b")
+        vec_rows = const.tile([P, P], BF16, name="vec_rows")
+        vec_cols = const.tile([P, P], BF16, name="vec_cols")
+        hold_b = const.tile([P, PITCHES], BF16, name="hold_b")
+        gain_b = const.tile([P, VOICES], BF16, name="gain_b")
+        keep_b = const.tile([P, GROUPS, SLOTS], BF16, name="keep_b")
+        first_copy = const.tile([P, 2], F32, name="first_copy")
 
-        def load_rows():
-            nc.sync.dma_start(out=rows[0:HR, :], in_=hold.rearrange("(c p) -> c p", p=P))
-            nc.sync.dma_start(out=rows[HR : HR + GR, :], in_=gain.rearrange("(c p) -> c p", p=P))
+        xr, cr, raw = {}, {}, {}
 
-        def spread_rows():
-            bank = psum.tile([P, P], BF16, name="rt", tag="bank")
-            nc.tensor.transpose(bank[:], rows[:], ident_b[:])
-            nc.scalar.copy(out=cols_b[:], in_=bank[:])
-            for k in range(NC + 1):
-                bank = psum.tile([P, K_PASS], BF16, name=f"rb{k}", tag="bank")
-                for i in range(T):
-                    c = T * k + i
-                    nc.tensor.transpose(
-                        bank[:, i * P : (i + 1) * P], cols_b[:, c : c + 1].to_broadcast([P, P]), ident_b[:]
-                    )
-                dst = hold_b[:, k * K_PASS : (k + 1) * K_PASS] if k < NC else gain_b[:]
+        def load_x(g, pair, slots):
+            if (g, pair) not in xr:
+                xr[g, pair] = const.tile([P, 2, PITCHES], BF16, name=f"x{g}{pair}")
+            lo, hi = slots[0], slots[-1] + 1
+            nc.sync.dma_start(out=xr[g, pair][:, lo:hi, :], in_=x_rows[g][:, 2 * pair + lo : 2 * pair + hi, :])
+
+        def load_cont(g, pair):
+            cr[g, pair] = work.tile([P, 2, BARS], BF16, name=f"cont{g}{pair}", tag="raw", bufs=10)
+            nc.sync.dma_start(out=cr[g, pair][:], in_=cont_rows[g][:, 2 * pair : 2 * pair + 2, :])
+
+        def load_kfirst(n, c):
+            raw[n, c] = work.tile([P, SLOTS, PASS], BF16, name=f"raw{n}{c}", tag="raw", bufs=10)
+            rows = dbl_rows[c] if n == DBL else sub_rows[c][:, :, n * PASS : (n + 1) * PASS]
+            nc.sync.dma_start(out=raw[n, c][:], in_=rows)
+
+        def load_keep():
+            nc.sync.dma_start(out=keep_b[:], in_=keep.rearrange("(g p t) -> p g t", g=GROUPS, t=SLOTS))
+
+        def load_hold_gain():
+            split = PITCHES // P
+            nc.vector.memset(vec_rows[:], 0.0)
+            nc.sync.dma_start(out=vec_rows[0:split, :], in_=hold.rearrange("(i q) -> i q", q=P))
+            nc.sync.dma_start(out=vec_rows[split : split + VOICES // P, :], in_=gain.rearrange("(i q) -> i q", q=P))
+
+        def spread_hold_gain():
+            bank = psum.tile([P, P], BF16, name="vec_turned", tag="bank")
+            nc.tensor.transpose(bank[:], vec_rows[:], ident_b[:])
+            nc.scalar.copy(out=vec_cols[:], in_=bank[:])
+            for n in range(CHUNKS + 1):
+                bank = psum.tile([P, PASS], BF16, name=f"vec_spread{n}", tag="bank")
+                for i in range(SLOTS):
+                    col = vec_cols[:, SLOTS * n + i : SLOTS * n + i + 1]
+                    nc.tensor.transpose(bank[:, i * P : (i + 1) * P], col.to_broadcast([P, P]), ident_b[:])
+                dst = hold_b[:, n * PASS : (n + 1) * PASS] if n < CHUNKS else gain_b[:]
                 nc.scalar.copy(out=dst, in_=bank[:])
 
-        def load_piece(n, c):
-            t = work.tile([P, T, K_PASS], BF16, name=f"raw{n}{c}", tag="raw", bufs=10)
-            nc.sync.dma_start(out=t[:], in_=sub_v[c][:, :, n * K_PASS : (n + 1) * K_PASS] if n < NC else dbl_v[c])
-            sr[n, c] = t[:]
+        grouped, codes = {}, {}
 
-        def load_cont(g, pr):
-            t = work.tile([P, 2, B], BF16, name=f"cr{g}{pr}", tag="raw", bufs=10)
-            nc.sync.dma_start(out=t[:], in_=cont_v[g][:, 2 * pr : 2 * pr + 2, :])
-            cr[g, pr] = t
+        def group_tile(key):
+            if key not in grouped:
+                grouped[key] = work.tile([P, PASS, SLOTS], BF16, name="g_" + key, tag="grouped", bufs=8, align_bytes=64)
+            return grouped[key]
 
-        def codes(key, tag, bufs):
-            q = work.tile([P, K_PASS], U32, name="q" + key, tag="q" + tag, bufs=bufs, align_bytes=64)
-            s = work.tile([P, K_PASS], U8, name="s" + key, tag="s" + tag, bufs=bufs, align_bytes=64)
-            return q, s
-
-        def grouped(key):
-            return work.tile([P, K_PASS, T], BF16, name="g" + key, tag="grouped", bufs=8, align_bytes=64)
-
-        def quantize(g, q):
+        def quantize(key, tag, bufs):
+            q = work.tile([P, PASS], U32, name="q_" + key, tag="q_" + tag, bufs=bufs, align_bytes=64)
+            s = work.tile([P, PASS], U8, name="s_" + key, tag="s_" + tag, bufs=bufs, align_bytes=64)
             nc.vector.quantize_mx(
-                out=q[0][:].bitcast(FP8X4), scales=q[1][:], in_=g[:].rearrange("p r j -> p (r j)")
+                out=q[:].bitcast(FP8X4), scales=s[:], in_=grouped[key][:].rearrange("p n j -> p (n j)")
             )
+            codes[key] = (q, s)
 
-        def mx(acc, lhs, m0, rhs, start, stop):
+        def multiply(acc, stationary, slot, moving, start, stop):
+            cols = slice(slot * P, (slot + 1) * P)
             nc.tensor.matmul_mx(
                 out=acc[:],
-                lhsT=lhs[0][:, m0 : m0 + P].bitcast(FP8X4),
-                lhsT_scale=lhs[1][:, m0 : m0 + P],
-                rhs=rhs[0][:].bitcast(FP8X4),
-                rhs_scale=rhs[1][:],
+                lhsT=codes[stationary][0][:, cols].bitcast(FP8X4),
+                lhsT_scale=codes[stationary][1][:, cols],
+                rhs=codes[moving][0][:].bitcast(FP8X4),
+                rhs_scale=codes[moving][1][:],
                 start=start,
                 stop=stop,
             )
 
-        ys, gx, xq, gc, cq, gs, sq, h, gh, hq, cb, gq, dq = {}, {}, {}, {}, {}, {}, {}, {}, {}, {}, {}, {}, {}
-
-        def turn(words, key, dst, dst_q, pr, step):
-            bank = psum.tile([P, 2, 2 * P], F32, name="tp" + key, tag="bank")
-            for tt in range(2):
+        def turn(key, rows, pair):
+            bank = psum.tile([P, 2, 2 * P], F32, name=f"t_{key}_{pair}", tag="bank")
+            for i in range(2):
+                words = rows[i].bitcast(F32)
                 for u in range(2):
-                    w = words[tt]
-                    src = w[:, u : 2 * P : 2] if step == 2 else w[:, u * P : (u + 1) * P]
-                    nc.tensor.transpose(bank[:, u, tt * P : (tt + 1) * P], src, ident[:])
-            nc.scalar.copy(
-                out=dst[:].rearrange("p r j -> p (r j)").bitcast(F32).rearrange("p (r u) -> p r u", u=2)[
-                    :, pr * 2 * P : (pr + 1) * 2 * P, :
-                ],
-                in_=bank[:].rearrange("p u r -> p r u"),
-            )
+                    nc.tensor.transpose(bank[:, u, i * P : (i + 1) * P], words[:, u : 2 * P : 2], ident[:])
+            dst = group_tile(key)[:].rearrange("p n j -> p (n j)").bitcast(F32).rearrange("p (n u) -> p n u", u=2)
+            nc.scalar.copy(out=dst[:, pair * 2 * P : (pair + 1) * 2 * P, :], in_=bank[:].rearrange("p u n -> p n u"))
 
-        def turn_x(g, pr, c):
-            if (g, c) not in gx:
-                gx[g, c] = grouped(f"x{g}{c}")
-            w = [xr[g, pr][:, tt, c * K_PASS : (c + 1) * K_PASS].bitcast(F32) for tt in range(2)]
-            turn(w, f"x{g}{pr}{c}", gx[g, c], None, pr, 2)
+        def turn_x(g):
+            for pair in BOTH:
+                for c in range(CHUNKS):
+                    turn(f"x{g}{c}", [xr[g, pair][:, i, c * PASS : (c + 1) * PASS] for i in range(2)], pair)
 
-        def q_x(g, c):
-            xq[g, c] = codes(f"x{g}{c}", "x", 6)
-            quantize(gx[g, c], xq[g, c])
+        def turn_cont(go):
+            for pair in BOTH:
+                for gi in range(GROUPS):
+                    turn(f"cont{go}{gi}", [cr[go, pair][:, i, gi * PASS : (gi + 1) * PASS] for i in range(2)], pair)
 
-        def turn_cont(go, gi, pr):
-            if (go, gi) not in gc:
-                gc[go, gi] = grouped(f"c{go}{gi}")
-            w = [cr[go, pr][:, tt, gi * K_PASS : (gi + 1) * K_PASS].bitcast(F32) for tt in range(2)]
-            turn(w, f"c{go}{gi}{pr}", gc[go, gi], None, pr, 2)
+        def turn_c(n, g):
+            for pair in BOTH:
+                turn(f"c{n}{g}", [c_rows[n, g][:, 2 * pair + i, :] for i in range(2)], pair)
 
-        def q_cont(go, gi):
-            cq[go, gi] = codes(f"c{go}{gi}", "c", 4)
-            quantize(gc[go, gi], cq[go, gi])
-
-        def inter(n, c, eng):
-            gs[n, c] = grouped(f"s{n}{c}")
-            if True:
-                for k in range(2):
-                    cols = slice(k * (K_PASS // 2), (k + 1) * (K_PASS // 2))
-                    o = gs[n, c][:, cols, :].rearrange("p (q i) j -> p q j i", i=4)
-                    i = sr[n, c][:, :, cols].rearrange("p j (q i) -> p q j i", i=4)
-                    if eng == "v":
-                        nc.vector.tensor_copy(out=o, in_=i)
-                    else:
-                        nc.scalar.copy(out=o, in_=i)
-
-        def q_s(n, c):
-            sq[n, c] = codes(f"s{n}{c}", "s" if n < 3 else "d", 6 if n < 3 else 3)
-            quantize(gs[n, c], sq[n, c])
-
-        def held(n, g, pr):
-            if (n, g) not in h:
-                h[n, g] = work.tile([P, T, K_PASS], F32, name=f"h{n}{g}", tag="h", bufs=6)
-            cols = slice(n * K_PASS, (n + 1) * K_PASS)
-            eng = nc.gpsimd if (False) else nc.vector
-            eng.tensor_tensor(
-                out=h[n, g][:, 2 * pr : 2 * pr + 2, :],
-                in0=xr[g, pr][:, :, cols],
-                in1=hold_b[:, cols].unsqueeze(1).to_broadcast([P, 2, K_PASS]),
-                op=ALU.mult,
-            )
-
-
-        def acc_tile(key):
-            return psum.tile([P, K_PASS], F32, name="acc" + key, tag="bank")
-
-        def add_relu(n, g, t, acc):
-            nc.vector.scalar_tensor_tensor(
-                out=h[n, g][:, t, :], in0=acc[:], scalar=0.0, in1=h[n, g][:, t, :], op0=ALU.max, op1=ALU.add
-            )
-
-        def s1(n, g, t):
-            acc = acc_tile(f"r{n}{g}{t}")
-            for c in range(NC):
-                mx(acc, xq[g, c], t * P, sq[n, c], c == 0, c == NC - 1)
-            add_relu(n, g, t, acc)
-
-        def cast_h(n, g):
-            gh[n, g] = grouped(f"h{n}{g}")
-            for half in range(2):
-                lo, hi = half * 2 * P, (half + 1) * 2 * P
-                nc.scalar.copy(
-                    out=gh[n, g][:, lo:hi, :].rearrange("p (q i) t -> p q t i", i=4),
-                    in_=h[n, g][:, :, lo:hi].rearrange("p t (q i) -> p q t i", i=4),
+        def interleave(n, c, copy):
+            for half in BOTH:
+                cols = slice(half * 2 * P, (half + 1) * 2 * P)
+                copy(
+                    out=group_tile(f"w{n}{c}")[:, cols, :].rearrange("p (m i) j -> p m j i", i=4),
+                    in_=raw[n, c][:, :, cols].rearrange("p j (m i) -> p m j i", i=4),
                 )
 
-        def q_h(n, g):
-            hq[n, g] = codes(f"h{n}{g}", "h", 4)
-            quantize(gh[n, g], hq[n, g])
+        def quantize_x(g):
+            for c in range(CHUNKS):
+                quantize(f"x{g}{c}", "x", GROUPS * CHUNKS)
 
-        def s2(n, go, t):
-            acc = acc_tile(f"m{n}{go}{t}")
-            for gi in range(NG):
-                mx(acc, cq[go, gi], t * P, hq[n, gi], gi == 0, gi == NG - 1)
-            if (n, go) not in cb:
-                cb[n, go] = work.tile([P, T, K_PASS], BF16, name=f"cb{n}{go}", tag="cb", bufs=2)
-            nc.vector.scalar_tensor_tensor(
-                out=cb[n, go][:, t, :],
-                in0=h[n, go][:, t, :],
-                scalar=keep_b[:, go, t : t + 1],
-                in1=acc[:],
-                op0=ALU.mult,
-                op1=ALU.add,
-            )
+        def quantize_cont(go, gi):
+            quantize(f"cont{go}{gi}", "cont", GROUPS * GROUPS)
 
-        def turn_c(n, go, pr):
-            if (n, go) not in gq:
-                gq[n, go] = grouped(f"q{n}{go}")
-            w = [cb[n, go][:, 2 * pr + tt, :].bitcast(F32) for tt in range(2)]
-            turn(w, f"q{n}{go}{pr}", gq[n, go], None, pr, 2)
+        def quantize_w(n, c):
+            quantize(f"w{n}{c}", "dbl" if n == DBL else "sub", CHUNKS if n == DBL else 2 * CHUNKS)
 
-        def q_c(n, go):
-            dq[n, go] = codes(f"q{n}{go}", "q", 6)
-            quantize(gq[n, go], dq[n, go])
+        def quantize_h(n, g):
+            quantize(f"h{n}{g}", "h", 2 * GROUPS)
 
-        ay = {}
+        def quantize_c(n, g):
+            quantize(f"c{n}{g}", "c", CHUNKS * GROUPS)
 
-        def s3_part(go, t, passes):
-            if passes[0] == 0:
-                ay[go, t] = acc_tile(f"y{go}{t}")
-            for n in passes:
-                mx(ay[go, t], dq[n, go], t * P, sq[3, n], n == 0, n == NC - 1)
+        h, c_rows, acc = {}, {}, {}
 
-        def s3_out(go, t):
-            if go not in ys:
-                ys[go] = work.tile([P, T, V], F32, name=f"y{go}", tag="h", bufs=6)
-            nc.vector.tensor_tensor(out=ys[go][:, t, :], in0=ay[go, t][:], in1=gain_b[:], op=ALU.mult)
-            nc.sync.dma_start(out=out_v[go][:, t, :], in_=ys[go][:, t, :])
+        def acc_tile(key):
+            acc[key] = psum.tile([P, PASS], F32, name="acc_%s%d%d%d" % key, tag="bank")
 
-        G = nc.gpsimd
-        nc.vector.memset(rows[:], 0.0)
-        load_rows()
-        loads = (
-            [(load_x, 0, 0), (load_x, 0, 1)]
-            + [(load_piece, 0, c) for c in range(NC)]
-            + [(load_x, 1, 0), (load_x, 1, 1)]
-            + [(load_piece, 1, c) for c in range(NC)]
-            + [(load_cont, 0, 0), (load_cont, 0, 1), (load_cont, 1, 0), (load_cont, 1, 1)]
-        )
-        for f, *a in loads:
-            f(*a)
-        nc.sync.dma_start(out=keep_b[:], in_=keep.rearrange("(g p t) -> p g t", g=NG, t=T))
+        def hold_x(n, g, pair, singly=False):
+            if (n, g) not in h:
+                h[n, g] = work.tile([P, SLOTS, PASS], F32, name=f"h{n}{g}", tag="h", bufs=CHUNKS * GROUPS)
+            cols = slice(n * PASS, (n + 1) * PASS)
+            for lo, hi in [(0, 1), (1, 2)] if singly else [(0, 2)]:
+                nc.vector.tensor_tensor(
+                    out=h[n, g][:, 2 * pair + lo : 2 * pair + hi, :],
+                    in0=xr[g, pair][:, lo:hi, cols],
+                    in1=hold_b[:, cols].unsqueeze(1).to_broadcast([P, hi - lo, PASS]),
+                    op=ALU.mult,
+                )
 
-        nc.vector.memset(warm[:], 0.0)
-        nc.scalar.copy(out=warm[:, 0:1], in_=warm[:, 1:2])
+        def stage1(n, g):
+            for t in range(SLOTS):
+                acc_tile(("r", n, g, t))
+                for c in range(CHUNKS):
+                    multiply(acc["r", n, g, t], f"x{g}{c}", t, f"w{n}{c}", c == 0, c == CHUNKS - 1)
+
+        def stage1_by_pass(n, g):
+            for c in range(CHUNKS):
+                for t in range(SLOTS):
+                    if c == 0:
+                        acc_tile(("r", n, g, t))
+                    multiply(acc["r", n, g, t], f"x{g}{c}", t, f"w{n}{c}", c == 0, c == CHUNKS - 1)
+
+        def add_relu(n, g):
+            for t in range(SLOTS):
+                slot = h[n, g][:, t, :]
+                nc.vector.scalar_tensor_tensor(
+                    out=slot, in0=acc["r", n, g, t][:], scalar=0.0, in1=slot, op0=ALU.max, op1=ALU.add
+                )
+
+        def round_h(n, g):
+            for half in BOTH:
+                cols = slice(half * 2 * P, (half + 1) * 2 * P)
+                nc.scalar.copy(
+                    out=group_tile(f"h{n}{g}")[:, cols, :].rearrange("p (m i) t -> p m t i", i=4),
+                    in_=h[n, g][:, :, cols].rearrange("p t (m i) -> p m t i", i=4),
+                )
+
+        def stage2(n, go):
+            for t in range(SLOTS):
+                acc_tile(("m", n, go, t))
+                for gi in range(GROUPS):
+                    multiply(acc["m", n, go, t], f"cont{go}{gi}", t, f"h{n}{gi}", gi == 0, gi == GROUPS - 1)
+
+        def add_kept(n, go):
+            c_rows[n, go] = work.tile([P, SLOTS, PASS], BF16, name=f"c{n}{go}", tag="c_rows", bufs=2)
+            for t in range(SLOTS):
+                nc.vector.scalar_tensor_tensor(
+                    out=c_rows[n, go][:, t, :],
+                    in0=h[n, go][:, t, :],
+                    scalar=keep_b[:, go, t : t + 1],
+                    in1=acc["m", n, go, t][:],
+                    op0=ALU.mult,
+                    op1=ALU.add,
+                )
+
+        def stage3(g, chunks):
+            for t in range(SLOTS):
+                if chunks[0] == 0:
+                    acc_tile(("y", 0, g, t))
+                for n in chunks:
+                    multiply(acc["y", 0, g, t], f"c{n}{g}", t, f"w{DBL}{n}", n == 0, n == CHUNKS - 1)
+
+        def store(g):
+            y = work.tile([P, SLOTS, VOICES], F32, name=f"y{g}", tag="h", bufs=CHUNKS * GROUPS)
+            for t in range(SLOTS):
+                nc.vector.tensor_tensor(out=y[:, t, :], in0=acc["y", 0, g, t][:], in1=gain_b[:], op=ALU.mult)
+                nc.sync.dma_start(out=out_rows[g][:, t, :], in_=y[:, t, :])
+
+        vector, scalar = nc.vector.tensor_copy, nc.scalar.copy
+        load_hold_gain()
+        nc.vector.memset(first_copy[:], 0.0)
+        nc.scalar.copy(out=first_copy[:, 0:1], in_=first_copy[:, 1:2])
         make_identity(nc, ident_b[:])
         make_identity(nc, ident[:])
-        spread_rows()
 
+        for c in (0, 2, 1):
+            load_kfirst(0, c)
+        load_x(0, 0, [0])
+        load_x(0, 0, [1])
+        load_x(0, 1, [0, 1])
+        load_x(1, 0, [0, 1])
+        load_x(1, 1, [0, 1])
+        for c in (2, 0, 1):
+            load_kfirst(1, c)
+        spread_hold_gain()
+        interleave(0, 2, scalar)
+        interleave(0, 0, vector)
+        quantize_w(0, 0)
+        interleave(0, 1, scalar)
+        turn_x(0)
+        hold_x(0, 0, 0, singly=True)
+        hold_x(2, 0, 0)
+        hold_x(1, 0, 0)
+        hold_x(0, 0, 1)
+        quantize_w(0, 2)
+        hold_x(0, 1, 0)
+        turn_x(1)
+        quantize_x(0)
+        quantize_w(0, 1)
+        interleave(1, 1, scalar)
+        hold_x(0, 1, 1)
 
-        for pr in range(2):
-            for c in range(NC):
-                turn_x(0, pr, c)
-            held(0, 0, pr)
-            if pr == 0:
-                held(1, 0, 0)
-        inter(0, 0, "v")
-        inter(0, 1, "s")
-        inter(0, 2, "s")
-        q_x(0, 0)
-        q_s(0, 0)
-        q_x(0, 1)
-        q_x(0, 2)
-        q_s(0, 1)
-        held(1, 0, 1)
-        held(0, 1, 0)
-        q_s(0, 2)
-        acc0 = [acc_tile(f"r00{t}") for t in range(T)]
-        for c in range(NC):
-            for t in range(T):
-                mx(acc0[t], xq[0, c], t * P, sq[0, c], c == 0, c == NC - 1)
-        for pr in range(2):
-            for c in range(NC):
-                turn_x(1, pr, c)
-        for t in range(T):
-            add_relu(0, 0, t, acc0[t])
-        held(0, 1, 1)
-        for c in range(NC):
-            load_piece(2, c)
-        for c in range(NC):
-            q_x(1, c)
-        inter(1, 0, "s")
-        cast_h(0, 0)
-        inter(1, 1, "s")
-        for t in range(T):
-            s1(0, 1, t)
-            if t % 2 == 0:
-                held(1, 1, t // 2)
-        q_h(0, 0)
-        q_s(1, 0)
-        inter(1, 2, "s")
-        q_s(1, 1)
-        for go in range(NG):
-            for pr in range(2):
-                for gi in range(NG):
-                    turn_cont(go, gi, pr)
-            if go == 0:
-                cast_h(0, 1)
-        q_s(1, 2)
-        tiles = [(g, t) for g in range(NG) for t in range(T)]
-        at = {}
+        stage1_by_pass(0, 0)
+        interleave(1, 2, scalar)
+        quantize_x(1)
+        add_relu(0, 0)
+        stage1(0, 1)
+        interleave(1, 0, scalar)
+        hold_x(1, 0, 1)
+        quantize_w(1, 1)
+        for pair in BOTH:
+            load_cont(0, pair)
+        for n in (2, DBL):
+            for c in range(CHUNKS):
+                load_kfirst(n, c)
+        add_relu(0, 1)
+        quantize_w(1, 0)
+        round_h(0, 0)
+        hold_x(2, 0, 1)
+        turn_cont(0)
+        round_h(0, 1)
+        interleave(2, 2, scalar)
+        for pair in BOTH:
+            load_cont(1, pair)
+        load_keep()
+        quantize_w(1, 2)
+        hold_x(1, 1, 0)
 
-        def later(i, f, *a):
-            at.setdefault(i, []).append((f, a))
+        stage1(1, 0)
+        stage1(1, 1)
+        quantize_h(0, 0)
+        hold_x(1, 1, 1)
+        add_relu(1, 0)
+        quantize_cont(0, 1)
+        interleave(2, 0, scalar)
+        quantize_h(0, 1)
+        quantize_cont(0, 0)
+        stage2(0, 0)
+        add_relu(1, 1)
+        interleave(2, 1, scalar)
+        add_kept(0, 0)
+        quantize_w(2, 2)
+        turn_cont(1)
+        quantize_w(2, 0)
+        quantize_w(2, 1)
+        round_h(1, 1)
+        turn_c(0, 0)
+        hold_x(2, 1, 0)
+        hold_x(2, 1, 1)
+        quantize_cont(1, 0)
 
-        for n in range(1, NC + 1):
-            s = 8 * n
-            if n < NC:
-                for g in range(NG):
-                    later(s + 4 * g + 3, cast_h, n, g)
-                    later(s + 4 * g + 3 + 2, q_h, n, g)
-            if n + 1 < NC:
-                for c in range(NC):
-                    later(s + 0 + 2 * c, inter, n + 1, c, "s")
-                    later(s + 0 + 2 * c + 1, q_s, n + 1, c)
-            if n + 1 < NC:
-                for g in range(NG):
-                    for pr in range(2):
-                        later(s + 0 + 4 * g + 2 * pr, held, n + 1, g, pr)
-            for g in range(NG):
-                for pr in range(2):
-                    later(s + 3 + 4 * g + (2 * pr + 1 if n == NC and g == 1 else 3) + 2, turn_c, n - 1, g, pr)
-                later(s + 3 + 4 * g + 3 + 2 + 1, q_c, n - 1, g)
-        for t in range(T):
-            later(35 + t // 4, s3_part, 0, t, [0, 1])
-        for c in range(NC):
-            later(26 + 1 * c, inter, 3, c, "s")
-            later(26 + 1 * c + 1, q_s, 3, c)
-        later(8, q_cont, 0, 0)
-        later(8, q_cont, 0, 1)
-        later(9, q_h, 0, 1)
-        later(10, q_cont, 1, 0)
-        later(10, q_cont, 1, 1)
-        for c in range(NC):
-            later(12, load_piece, 3, c)
-        for i in range(8, 8 * (NC + 1) + 3 + 2 + 1 + 1):
-            if i < 8 * NC:
-                s1(i // 8, *tiles[i % 8])
-            j = i - 8 - 3
-            if 0 <= j < 8 * NC:
-                s2(j // 8, *tiles[j % 8])
-            for f, a in at.get(i, []):
-                f(*a)
-        for t in range(T):
-            s3_part(0, t, [2])
-            s3_out(0, t)
-        for t in range(T):
-            s3_part(1, t, [0, 1])
-        for t in range(T):
-            s3_part(1, t, [2])
-            s3_out(1, t)
+        stage1(2, 0)
+        add_relu(2, 0)
+        stage1(2, 1)
+        quantize_cont(1, 1)
+        stage2(0, 1)
+        add_relu(2, 1)
+        round_h(1, 0)
+        quantize_h(1, 0)
+        quantize_h(1, 1)
+        round_h(2, 0)
+        add_kept(0, 1)
+        round_h(2, 1)
+        stage2(1, 0)
+        interleave(DBL, 0, scalar)
+        add_kept(1, 0)
+        quantize_h(2, 0)
+        stage2(1, 1)
+        quantize_h(2, 1)
+        turn_c(0, 1)
+        interleave(DBL, 1, scalar)
+        add_kept(1, 1)
+        turn_c(1, 0)
+        quantize_c(0, 0)
+        quantize_w(DBL, 0)
+
+        stage2(2, 0)
+        turn_c(1, 1)
+        interleave(DBL, 2, scalar)
+        add_kept(2, 0)
+        stage2(2, 1)
+        quantize_w(DBL, 1)
+        add_kept(2, 1)
+        turn_c(2, 0)
+        quantize_c(1, 0)
+        quantize_c(1, 1)
+        quantize_c(2, 0)
+        turn_c(2, 1)
+        quantize_w(DBL, 2)
+        quantize_c(0, 1)
+        stage3(0, [0, 1])
+        quantize_c(2, 1)
+        stage3(0, [2])
+        store(0)
+        stage3(1, [0, 1])
+        stage3(1, [2])
+        store(1)

from contextlib import ExitStack

import concourse.mybir as mybir
from concourse.masks import make_identity

BARS, PITCHES, VOICES = 1024, 1536, 512
FLOPS = 2 * (BARS * PITCHES * PITCHES + BARS * BARS * PITCHES + BARS * PITCHES * VOICES)

F32 = mybir.dt.float32
BF16 = mybir.dt.bfloat16
U32 = mybir.dt.uint32
U8 = mybir.dt.uint8
FP8X4 = mybir.dt.float8_e4m3fn_x4
ALU = mybir.AluOpType

P = 128
SLOTS = 4
PASS = P * SLOTS
GROUPS = BARS // PASS
CHUNKS = PITCHES // PASS
DBL = CHUNKS
BOTH = range(2)


def tile_chord_substitution_continuity_doubli_t1_kernel(tc, x, sub, hold, cont, keep, dbl, gain, out):
    nc = tc.nc
    with ExitStack() as ctx:
        const = ctx.enter_context(tc.tile_pool(name="const", bufs=1))
        work = ctx.enter_context(tc.tile_pool(name="work", bufs=2))
        psum = ctx.enter_context(tc.psum_pool(name="psum", bufs=8))
        ctx.enter_context(tc.manual_schedule())

        x_rows = x.rearrange("(g p t) k -> g p t k", g=GROUPS, t=SLOTS)
        cont_rows = cont.rearrange("(g p t) k -> g p t k", g=GROUPS, t=SLOTS)
        out_rows = out.rearrange("(g p t) v -> g p t v", g=GROUPS, t=SLOTS)
        sub_rows = sub.rearrange("(c p j) w -> c p j w", c=CHUNKS, j=SLOTS)
        dbl_rows = dbl.rearrange("(c p j) v -> c p j v", c=CHUNKS, j=SLOTS)

        ident = const.tile([P, P], F32, name="ident")
        ident_b = const.tile([P, P], BF16, name="ident_b")
        vec_rows = const.tile([P, P], BF16, name="vec_rows")
        vec_cols = const.tile([P, P], BF16, name="vec_cols")
        hold_b = const.tile([P, PITCHES], BF16, name="hold_b")
        gain_b = const.tile([P, VOICES], BF16, name="gain_b")
        keep_b = const.tile([P, GROUPS, SLOTS], BF16, name="keep_b")
        first_copy = const.tile([P, 2], F32, name="first_copy")

        xr, cr, raw = {}, {}, {}

        def load_x(g, pair, slots):
            if (g, pair) not in xr:
                xr[g, pair] = const.tile([P, 2, PITCHES], BF16, name=f"x{g}{pair}")
            lo, hi = slots[0], slots[-1] + 1
            nc.sync.dma_start(out=xr[g, pair][:, lo:hi, :], in_=x_rows[g][:, 2 * pair + lo : 2 * pair + hi, :])

        def load_cont(g, pair):
            cr[g, pair] = work.tile([P, 2, BARS], BF16, name=f"cont{g}{pair}", tag="raw", bufs=10)
            nc.sync.dma_start(out=cr[g, pair][:], in_=cont_rows[g][:, 2 * pair : 2 * pair + 2, :])

        def load_kfirst(n, c):
            raw[n, c] = work.tile([P, SLOTS, PASS], BF16, name=f"raw{n}{c}", tag="raw", bufs=10)
            rows = dbl_rows[c] if n == DBL else sub_rows[c][:, :, n * PASS : (n + 1) * PASS]
            nc.sync.dma_start(out=raw[n, c][:], in_=rows)

        def load_keep():
            nc.sync.dma_start(out=keep_b[:], in_=keep.rearrange("(g p t) -> p g t", g=GROUPS, t=SLOTS))

        def load_hold_gain():
            split = PITCHES // P
            nc.vector.memset(vec_rows[:], 0.0)
            nc.sync.dma_start(out=vec_rows[0:split, :], in_=hold.rearrange("(i q) -> i q", q=P))
            nc.sync.dma_start(out=vec_rows[split : split + VOICES // P, :], in_=gain.rearrange("(i q) -> i q", q=P))

        def spread_hold_gain():
            bank = psum.tile([P, P], BF16, name="vec_turned", tag="bank")
            nc.tensor.transpose(bank[:], vec_rows[:], ident_b[:])
            nc.scalar.copy(out=vec_cols[:], in_=bank[:])
            for n in range(CHUNKS + 1):
                bank = psum.tile([P, PASS], BF16, name=f"vec_spread{n}", tag="bank")
                for i in range(SLOTS):
                    col = vec_cols[:, SLOTS * n + i : SLOTS * n + i + 1]
                    nc.tensor.transpose(bank[:, i * P : (i + 1) * P], col.to_broadcast([P, P]), ident_b[:])
                dst = hold_b[:, n * PASS : (n + 1) * PASS] if n < CHUNKS else gain_b[:]
                nc.scalar.copy(out=dst, in_=bank[:])

        grouped, codes = {}, {}

        def group_tile(key):
            if key not in grouped:
                grouped[key] = work.tile([P, PASS, SLOTS], BF16, name="g_" + key, tag="grouped", bufs=8, align_bytes=64)
            return grouped[key]

        def quantize(key, tag, bufs):
            q = work.tile([P, PASS], U32, name="q_" + key, tag="q_" + tag, bufs=bufs, align_bytes=64)
            s = work.tile([P, PASS], U8, name="s_" + key, tag="s_" + tag, bufs=bufs, align_bytes=64)
            nc.vector.quantize_mx(
                out=q[:].bitcast(FP8X4), scales=s[:], in_=grouped[key][:].rearrange("p n j -> p (n j)")
            )
            codes[key] = (q, s)

        def multiply(acc, stationary, slot, moving, start, stop):
            cols = slice(slot * P, (slot + 1) * P)
            nc.tensor.matmul_mx(
                out=acc[:],
                lhsT=codes[stationary][0][:, cols].bitcast(FP8X4),
                lhsT_scale=codes[stationary][1][:, cols],
                rhs=codes[moving][0][:].bitcast(FP8X4),
                rhs_scale=codes[moving][1][:],
                start=start,
                stop=stop,
            )

        def turn(key, rows, pair):
            bank = psum.tile([P, 2, 2 * P], F32, name=f"t_{key}_{pair}", tag="bank")
            for i in range(2):
                words = rows[i].bitcast(F32)
                for u in range(2):
                    nc.tensor.transpose(bank[:, u, i * P : (i + 1) * P], words[:, u : 2 * P : 2], ident[:])
            dst = group_tile(key)[:].rearrange("p n j -> p (n j)").bitcast(F32).rearrange("p (n u) -> p n u", u=2)
            nc.scalar.copy(out=dst[:, pair * 2 * P : (pair + 1) * 2 * P, :], in_=bank[:].rearrange("p u n -> p n u"))

        def turn_x(g):
            for pair in BOTH:
                for c in range(CHUNKS):
                    turn(f"x{g}{c}", [xr[g, pair][:, i, c * PASS : (c + 1) * PASS] for i in range(2)], pair)

        def turn_cont(go):
            for pair in BOTH:
                for gi in range(GROUPS):
                    turn(f"cont{go}{gi}", [cr[go, pair][:, i, gi * PASS : (gi + 1) * PASS] for i in range(2)], pair)

        def turn_c(n, g):
            for pair in BOTH:
                turn(f"c{n}{g}", [c_rows[n, g][:, 2 * pair + i, :] for i in range(2)], pair)

        def interleave(n, c, copy):
            for half in BOTH:
                cols = slice(half * 2 * P, (half + 1) * 2 * P)
                copy(
                    out=group_tile(f"w{n}{c}")[:, cols, :].rearrange("p (m i) j -> p m j i", i=4),
                    in_=raw[n, c][:, :, cols].rearrange("p j (m i) -> p m j i", i=4),
                )

        def quantize_x(g):
            for c in range(CHUNKS):
                quantize(f"x{g}{c}", "x", GROUPS * CHUNKS)

        def quantize_cont(go, gi):
            quantize(f"cont{go}{gi}", "cont", GROUPS * GROUPS)

        def quantize_w(n, c):
            quantize(f"w{n}{c}", "dbl" if n == DBL else "sub", CHUNKS if n == DBL else 2 * CHUNKS)

        def quantize_h(n, g):
            quantize(f"h{n}{g}", "h", 2 * GROUPS)

        def quantize_c(n, g):
            quantize(f"c{n}{g}", "c", CHUNKS * GROUPS)

        h, c_rows, acc = {}, {}, {}

        def acc_tile(key):
            acc[key] = psum.tile([P, PASS], F32, name="acc_%s%d%d%d" % key, tag="bank")

        def hold_x(n, g, pair, singly=False):
            if (n, g) not in h:
                h[n, g] = work.tile([P, SLOTS, PASS], F32, name=f"h{n}{g}", tag="h", bufs=CHUNKS * GROUPS)
            cols = slice(n * PASS, (n + 1) * PASS)
            for lo, hi in [(0, 1), (1, 2)] if singly else [(0, 2)]:
                nc.vector.tensor_tensor(
                    out=h[n, g][:, 2 * pair + lo : 2 * pair + hi, :],
                    in0=xr[g, pair][:, lo:hi, cols],
                    in1=hold_b[:, cols].unsqueeze(1).to_broadcast([P, hi - lo, PASS]),
                    op=ALU.mult,
                )

        def stage1(n, g):
            for t in range(SLOTS):
                acc_tile(("r", n, g, t))
                for c in range(CHUNKS):
                    multiply(acc["r", n, g, t], f"x{g}{c}", t, f"w{n}{c}", c == 0, c == CHUNKS - 1)

        def stage1_by_pass(n, g):
            for c in range(CHUNKS):
                for t in range(SLOTS):
                    if c == 0:
                        acc_tile(("r", n, g, t))
                    multiply(acc["r", n, g, t], f"x{g}{c}", t, f"w{n}{c}", c == 0, c == CHUNKS - 1)

        def add_relu(n, g):
            for t in range(SLOTS):
                slot = h[n, g][:, t, :]
                nc.vector.scalar_tensor_tensor(
                    out=slot, in0=acc["r", n, g, t][:], scalar=0.0, in1=slot, op0=ALU.max, op1=ALU.add
                )

        def round_h(n, g):
            for half in BOTH:
                cols = slice(half * 2 * P, (half + 1) * 2 * P)
                nc.scalar.copy(
                    out=group_tile(f"h{n}{g}")[:, cols, :].rearrange("p (m i) t -> p m t i", i=4),
                    in_=h[n, g][:, :, cols].rearrange("p t (m i) -> p m t i", i=4),
                )

        def stage2(n, go):
            for t in range(SLOTS):
                acc_tile(("m", n, go, t))
                for gi in range(GROUPS):
                    multiply(acc["m", n, go, t], f"cont{go}{gi}", t, f"h{n}{gi}", gi == 0, gi == GROUPS - 1)

        def add_kept(n, go):
            c_rows[n, go] = work.tile([P, SLOTS, PASS], BF16, name=f"c{n}{go}", tag="c_rows", bufs=2)
            for t in range(SLOTS):
                nc.vector.scalar_tensor_tensor(
                    out=c_rows[n, go][:, t, :],
                    in0=h[n, go][:, t, :],
                    scalar=keep_b[:, go, t : t + 1],
                    in1=acc["m", n, go, t][:],
                    op0=ALU.mult,
                    op1=ALU.add,
                )

        def stage3(g, chunks):
            for t in range(SLOTS):
                if chunks[0] == 0:
                    acc_tile(("y", 0, g, t))
                for n in chunks:
                    multiply(acc["y", 0, g, t], f"c{n}{g}", t, f"w{DBL}{n}", n == 0, n == CHUNKS - 1)

        def store(g):
            y = work.tile([P, SLOTS, VOICES], F32, name=f"y{g}", tag="h", bufs=CHUNKS * GROUPS)
            for t in range(SLOTS):
                nc.vector.tensor_tensor(out=y[:, t, :], in0=acc["y", 0, g, t][:], in1=gain_b[:], op=ALU.mult)
                nc.sync.dma_start(out=out_rows[g][:, t, :], in_=y[:, t, :])

        vector, scalar = nc.vector.tensor_copy, nc.scalar.copy
        load_hold_gain()
        nc.vector.memset(first_copy[:], 0.0)
        nc.scalar.copy(out=first_copy[:, 0:1], in_=first_copy[:, 1:2])
        make_identity(nc, ident_b[:])
        make_identity(nc, ident[:])

        for c in (0, 2, 1):
            load_kfirst(0, c)
        load_x(0, 0, [0])
        load_x(0, 0, [1])
        load_x(0, 1, [0, 1])
        load_x(1, 0, [0, 1])
        load_x(1, 1, [0, 1])
        for c in (2, 0, 1):
            load_kfirst(1, c)
        spread_hold_gain()
        interleave(0, 2, scalar)
        interleave(0, 0, vector)
        quantize_w(0, 0)
        interleave(0, 1, scalar)
        turn_x(0)
        hold_x(0, 0, 0, singly=True)
        hold_x(2, 0, 0)
        hold_x(1, 0, 0)
        hold_x(0, 0, 1)
        quantize_w(0, 2)
        hold_x(0, 1, 0)
        turn_x(1)
        quantize_x(0)
        quantize_w(0, 1)
        interleave(1, 1, scalar)
        hold_x(0, 1, 1)

        stage1_by_pass(0, 0)
        interleave(1, 2, scalar)
        quantize_x(1)
        add_relu(0, 0)
        stage1(0, 1)
        interleave(1, 0, scalar)
        hold_x(1, 0, 1)
        quantize_w(1, 1)
        for pair in BOTH:
            load_cont(0, pair)
        for n in (2, DBL):
            for c in range(CHUNKS):
                load_kfirst(n, c)
        add_relu(0, 1)
        quantize_w(1, 0)
        round_h(0, 0)
        hold_x(2, 0, 1)
        turn_cont(0)
        round_h(0, 1)
        interleave(2, 2, scalar)
        for pair in BOTH:
            load_cont(1, pair)
        load_keep()
        quantize_w(1, 2)
        hold_x(1, 1, 0)

        stage1(1, 0)
        stage1(1, 1)
        quantize_h(0, 0)
        hold_x(1, 1, 1)
        add_relu(1, 0)
        quantize_cont(0, 1)
        interleave(2, 0, scalar)
        quantize_h(0, 1)
        quantize_cont(0, 0)
        stage2(0, 0)
        add_relu(1, 1)
        interleave(2, 1, scalar)
        add_kept(0, 0)
        quantize_w(2, 2)
        turn_cont(1)
        quantize_w(2, 0)
        quantize_w(2, 1)
        round_h(1, 1)
        turn_c(0, 0)
        hold_x(2, 1, 0)
        hold_x(2, 1, 1)
        quantize_cont(1, 0)

        stage1(2, 0)
        add_relu(2, 0)
        stage1(2, 1)
        quantize_cont(1, 1)
        stage2(0, 1)
        add_relu(2, 1)
        round_h(1, 0)
        quantize_h(1, 0)
        quantize_h(1, 1)
        round_h(2, 0)
        add_kept(0, 1)
        round_h(2, 1)
        stage2(1, 0)
        interleave(DBL, 0, scalar)
        add_kept(1, 0)
        quantize_h(2, 0)
        stage2(1, 1)
        quantize_h(2, 1)
        turn_c(0, 1)
        interleave(DBL, 1, scalar)
        add_kept(1, 1)
        turn_c(1, 0)
        quantize_c(0, 0)
        quantize_w(DBL, 0)

        stage2(2, 0)
        turn_c(1, 1)
        interleave(DBL, 2, scalar)
        add_kept(2, 0)
        stage2(2, 1)
        quantize_w(DBL, 1)
        add_kept(2, 1)
        turn_c(2, 0)
        quantize_c(1, 0)
        quantize_c(1, 1)
        quantize_c(2, 0)
        turn_c(2, 1)
        quantize_w(DBL, 2)
        quantize_c(0, 1)
        stage3(0, [0, 1])
        quantize_c(2, 1)
        stage3(0, [2])
        store(0)
        stage3(1, [0, 1])
        stage3(1, [2])
        store(1)
